import numpy as np
import ml_dtypes


def mxq(x, axis, fmt="e4m3"):
    dtype, down = {"e4m3": (ml_dtypes.float8_e4m3fn, 7), "e5m2": (ml_dtypes.float8_e5m2, 14)}[fmt]
    v = np.moveaxis(np.asarray(x, np.float32).astype(ml_dtypes.bfloat16).astype(np.float64), axis, -1)
    blocks = v.reshape(v.shape[:-1] + (-1, 32))
    amax = np.abs(blocks).max(-1, keepdims=True)
    byte = np.maximum(np.where(amax > 0, np.frexp(amax)[1] - 1 + 127, 0) - down, 1)
    scale = np.exp2(byte - 127.0)
    codes = (blocks / scale).astype(np.float32).astype(dtype).astype(np.float64)
    return np.moveaxis((codes * scale).reshape(v.shape), -1, axis)


WIDE = False


def mx_kscale(k):
    if not WIDE:
        return np.ones(k)
    levels = np.array([30, -30])
    if k % 512:
        return np.exp2(np.random.permutation(np.resize(levels, k // 32))).repeat(32)
    a = np.empty((k // 512, 16))
    for p in range(k // 512):
        a[p, :8] = np.random.permutation(np.resize(levels, 8))
        for g in range(8):
            far = levels[np.abs(levels - a[p, g]) >= 10]
            a[p, g + 8] = far[np.random.randint(len(far))]
    return np.exp2(a.ravel()).repeat(32)


def f64(x):
    return np.asarray(x).astype(np.float64)


def striped(idx):
    return np.tile(idx.reshape(-1, 16).T, (8, 1)).astype(np.uint16)


def unstriped(offs):
    return offs[:16].T.reshape(-1).astype(np.int64)


def d_silu(v):
    s = 1.0 / (1.0 + np.exp(-np.maximum(v, -700.0)))
    return s * (1.0 + v * (1.0 - s))


K, T, E, C, H, N = 256, 2048, 4, 512, 512, 512


def by_expert(wq, xq):
    return np.concatenate([wq[e].T @ xq[:, e * C:(e + 1) * C] for e in range(E)], axis=1)


def setup_inputs():
    n = np.random.standard_normal
    slot_token = np.random.permutation(T)[:E * C]
    s = mx_kscale(N)[:, None]
    z = np.ones(T); z[slot_token] = mx_kscale(E * C)
    return {
        "xT": (n((K, T)) * z[None, :]).astype(np.float32),
        "dyT": (n((N, T)) * s).astype(np.float32),
        "a": n((H, E * C)).astype(np.float32),
        "w2": (n((E, N, H)) / np.sqrt(N) / s[None]).astype(np.float32),
        "gate": np.tile(np.random.uniform(0.2, 1.0, E * C) / z[slot_token], (N, 1)).astype(np.float32),
        "offs": striped(slot_token),
    }


def reference(xT, dyT, a, w2, gate, offs):
    idx = unstriped(offs)
    gq = mxq(f64(gate) * f64(dyT)[:, idx], 0, "e5m2")
    dh = by_expert(mxq(f64(w2), 1, "e4m3"), gq)
    da = mxq(dh * d_silu(f64(a)), 1, "e5m2")
    xq = mxq(f64(xT)[:, idx], 1, "e4m3")
    return np.stack([(xq[:, e * C:(e + 1) * C] @ da[:, e * C:(e + 1) * C].T) for e in range(E)])

@@ -1,0 +1,285 @@
+from contextlib import ExitStack
+
+import concourse.mybir as mybir
+from concourse.masks import make_identity
+
+K, T, E, C, H, N = 256, 2048, 4, 512, 512, 512
+FLOPS = 2 * E * C * H * (N + K)
+
+F32 = mybir.dt.float32
+BF16 = mybir.dt.bfloat16
+U32 = mybir.dt.uint32
+U16 = mybir.dt.uint16
+U8 = mybir.dt.uint8
+E4M3 = mybir.dt.float8_e4m3fn_x4
+E5M2 = mybir.dt.float8_e5m2_x4
+ALU = mybir.AluOpType
+ACT = mybir.ActivationFunctionType
+
+P = 128
+PACK = 4
+LIST = 16
+G_ON_VECTOR = ()
+
+
+def tile_moe_mlp_silu_kernel(tc, xT, dyT, a, w2, gate, offs, out):
+    nc = tc.nc
+    with ExitStack() as ctx:
+        held = ctx.enter_context(tc.tile_pool(name="held", bufs=1))
+        ring = ctx.enter_context(tc.tile_pool(name="ring", bufs=2))
+        psum = ctx.enter_context(tc.psum_pool(name="psum", bufs=2))
+
+        offsets = held.tile([P, E * C // LIST], U16, name="offsets")
+        ident = held.tile([P, P], F32, name="ident")
+        make_identity(nc, ident[:])
+
+        def slots(first, count):
+            return offsets[:, first // LIST : (first + count) // LIST]
+
+        dy = {}
+        gates = held.tile([P, E * C], F32, name="gates")
+        pre = [held.tile([P, PACK * C], F32, name=f"pre{e}") for e in range(E)]
+        g32 = [held.tile([P, PACK, 2 * C], F32, name=f"g32_{h}") for h in range(2)]
+        x_pairs = held.tile([P, 2 * T], BF16, name="x_pairs")
+        x_slots = [held.tile([P, 2 * C], U32, name=f"x_slots{h}") for h in range(2)]
+        raw = {}
+
+        dy_rows = dyT.rearrange("(p t) c -> p t c", t=PACK)
+        a_rows = a.rearrange("(b p) c -> p b c", p=P)
+        x_rows = xT.rearrange("(p j) c -> p j c", j=2)
+
+        def load_dy(t):
+            dy[t] = ring.tile([P, T], F32, name="raw", bufs=7)
+            nc.sync.dma_start(out=dy[t][:], in_=dy_rows[:, t, :])
+
+        gate_row = held.tile([P, E * C // P], F32, name="gate_row")
+
+        def spread_gate():
+            for r in range(4):
+                spread = psum.tile([P, 4 * P], F32, name="dh" if r < 2 else "acc", bufs=3)
+                for c in range(4):
+                    column = gate_row[:, 4 * r + c : 4 * r + c + 1].to_broadcast([P, P])
+                    nc.tensor.transpose(spread[:, c * P : (c + 1) * P], column, ident[:])
+                copy = nc.vector.tensor_copy if r % 2 == 0 else nc.scalar.copy
+                copy(
+                    out=gates[:].rearrange("p (q r c) -> p r q c", r=4, c=4)[:, r],
+                    in_=spread[:].rearrange("p (c q) -> p q c", c=4),
+                )
+
+        def load_a(e, first, count):
+            nc.sync.dma_start(
+                out=pre[e][:, first * C : (first + count) * C].rearrange("p (b c) -> p b c", b=count),
+                in_=a_rows[:, first : first + count, e * C : (e + 1) * C],
+            )
+
+        def load_w(e):
+            raw["w", e] = ring.tile([P, PACK * H], F32, name="raw", bufs=7)
+            nc.sync.dma_start(out=raw["w", e][:], in_=w2[e].rearrange("(p t) i -> p (t i)", t=PACK))
+
+        def load_x(h):
+            raw["x", h] = ring.tile([P, T], F32, name="raw", bufs=7)
+            nc.sync.dma_start(
+                out=raw["x", h][:].rearrange("p (j c) -> p j c", j=2), in_=x_rows[:, :, h * T // 2 : (h + 1) * T // 2]
+            )
+
+        rest = {}
+
+        def activations(e, cuts=(0, 4)):
+            rest[e] = ring.tile([P, 4 * C], F32, name="rest", bufs=3)
+            for first, last in zip(cuts, cuts[1:]):
+                part = slice(first * C, last * C)
+                nc.scalar.activation(rest[e][:, part], pre[e][:, part], ACT.Silu, scale=-1.0)
+                nc.scalar.activation(pre[e][:, part], pre[e][:, part], ACT.Tanh, scale=-0.5)
+
+        def gather_dy(t, first, count):
+            h, at = divmod(first, 2 * C)
+            nc.vector.tensor_tensor(
+                g32[h][:, t, at : at + count], dy[t][:].indirect(slots(first, count)), gates[:, first : first + count], ALU.mult
+            )
+
+        def weave(copy, dst, src):
+            copy(
+                out=dst.rearrange("p (c i t) -> p c t i", i=4, t=PACK),
+                in_=src.rearrange("p t (c i) -> p c t i", i=4),
+            )
+
+        def quantise(src, fmt, tag, bufs):
+            width = src.shape[1] // PACK
+            codes = ring.tile([P, width], U32, name=tag + "_codes", align_bytes=64, bufs=bufs)
+            scales = ring.tile([P, width], U8, name=tag + "_scales", align_bytes=64, bufs=bufs)
+            nc.vector.quantize_mx(out=codes[:].bitcast(fmt), scales=scales[:], in_=src)
+            return codes, scales
+
+        wq, gq, xq, da_t = {}, {}, {}, {}
+
+        def weights(e):
+            wb = ring.tile([P, PACK * H], BF16, name="wb", align_bytes=64)
+            weave(nc.scalar.copy, wb[:], raw["w", e][:].rearrange("p (t i) -> p t i", t=PACK))
+            return lambda: wq.update({e: quantise(wb[:], E4M3, "w", 2)})
+
+        def grads(e):
+            gb = ring.tile([P, PACK * C], BF16, name="gb", align_bytes=64)
+            h, at = divmod(e * C, 2 * C)
+            copy = nc.vector.tensor_copy if e in G_ON_VECTOR else nc.scalar.copy
+            weave(copy, gb[:], g32[h][:, :, at : at + C])
+            return lambda: gq.update({e: quantise(gb[:], E5M2, "g", 2)})
+
+        def cast_x(h):
+            nc.scalar.copy(
+                out=x_pairs[:, h * T : (h + 1) * T].rearrange("p (c i j) -> p c j i", i=4, j=2),
+                in_=raw["x", h][:].rearrange("p (j c i) -> p c j i", i=4, j=2),
+            )
+
+        def gather_x(h):
+            nc.vector.tensor_copy(x_slots[h][:], x_pairs[:].bitcast(U32).indirect(slots(h * 2 * C, 2 * C)))
+
+        def tokens(e):
+            h, at = divmod(e * C, 2 * C)
+            words = x_slots[h][:].bitcast(F32)
+            turned = psum.tile([P, PACK * P], F32, name="acc", bufs=3)
+            for t in range(PACK):
+                nc.tensor.transpose(turned[:, t * P : (t + 1) * P], words[:, at + t : at + C : PACK], ident[:])
+            xb = ring.tile([P, PACK * K], BF16, name="xb", align_bytes=64)
+            nc.scalar.copy(
+                out=xb[:].rearrange("p (k t) -> p k t", t=PACK),
+                in_=turned[:].bitcast(BF16).rearrange("p (t k) -> p k t", t=PACK),
+            )
+            xq[e] = quantise(xb[:], E4M3, "x", 4)
+
+        turned_da = {}
+
+        def slope(e, h):
+            da = ring.tile([P, 2 * C], BF16, name="da", bufs=4)
+            sums = []
+            for b in range(2):
+                cols = slice((2 * h + b) * P, (2 * h + b + 1) * P)
+                dh = psum.tile([P, C], F32, name="dh", bufs=3)
+                nc.tensor.matmul_mx(
+                    out=dh[:], lhsT=wq[e][0][:, cols].bitcast(E4M3), lhsT_scale=wq[e][1][:, cols],
+                    rhs=gq[e][0][:].bitcast(E5M2), rhs_scale=gq[e][1][:], start=True, stop=True,
+                )
+                sums.append(dh)
+            for b in range(2):
+                part = slice(b * C, (b + 1) * C)
+                nc.vector.scalar_tensor_tensor(
+                    rest[e][:, 2 * h * C :][:, part], rest[e][:, 2 * h * C :][:, part], 1.0, sums[b][:], ALU.subtract, ALU.mult
+                )
+            words = da[:].bitcast(F32)
+            turned_da[e, h] = []
+            for blocks in [(0,), (1,)] if (e, h) == (E - 1, 1) else [(0, 1)]:
+                part = slice(blocks[0] * C, (blocks[-1] + 1) * C)
+                nc.vector.scalar_tensor_tensor(
+                    da[:, part], pre[e][:, 2 * h * C :][:, part], 1.0, rest[e][:, 2 * h * C :][:, part], ALU.subtract, ALU.mult
+                )
+                turned = psum.tile([P, 2 * len(blocks) * P], F32, name="da_turned")
+                for b in blocks:
+                    for u in range(2):
+                        q = 2 * (b - blocks[0]) + u
+                        nc.tensor.transpose(
+                            turned[:, q * P : (q + 1) * P], words[:, b * C // 2 + u : (b + 1) * C // 2 : 2], ident[:]
+                        )
+                turned_da[e, h].append((2 * h + blocks[0], len(blocks), turned))
+                if len(blocks) == 1:
+                    collect(e, h)
+
+        def collect(e, h):
+            if h == 0:
+                da_t[e] = ring.tile([P, PACK * H], BF16, name="da_t", align_bytes=64)
+            first, count, turned = turned_da[e, h].pop()
+            nc.scalar.copy(
+                out=da_t[e][:, first * PACK * P : (first + count) * PACK * P].bitcast(F32).rearrange("p (b i u) -> p b i u", i=P, u=2),
+                in_=turned[:].rearrange("p (b u i) -> p b i u", i=P, u=2),
+            )
+
+        def back(e):
+            codes = ring.tile([P, H], U32, name="da_codes", align_bytes=64)
+            scales = ring.tile([P, H], U8, name="da_scales", align_bytes=64)
+            for cols in [slice(0, 2 * P), slice(2 * P, 3 * P), slice(3 * P, H)] if e == E - 1 else [slice(0, H)]:
+                nc.vector.quantize_mx(
+                    out=codes[:, cols].bitcast(E5M2),
+                    scales=scales[:, cols],
+                    in_=da_t[e][:, cols.start * PACK : cols.stop * PACK],
+                )
+            result = ring.tile([P, K // P * H], F32, name="raw", bufs=7)
+            for kb in range(K // P):
+                cols = slice(kb * P, (kb + 1) * P)
+                part = result[:, kb * H : (kb + 1) * H]
+                acc = psum.tile([P, H], F32, name="dh", bufs=3) if e == E - 1 else psum.tile([P, H], F32, name="acc", bufs=3)
+                nc.tensor.matmul_mx(
+                    out=acc[:], lhsT=xq[e][0][:, cols].bitcast(E4M3), lhsT_scale=xq[e][1][:, cols],
+                    rhs=codes[:].bitcast(E5M2), rhs_scale=scales[:], start=True, stop=True,
+                )
+                if e == E - 1 and kb == 1:
+                    nc.vector.tensor_scalar_mul(part, acc[:], 0.5)
+                else:
+                    nc.scalar.activation(part, acc[:], ACT.Copy, scale=0.5)
+                nc.sync.dma_start(out=out[e, cols, :], in_=part)
+
+        nc.sync.dma_start(out=gate_row[:], in_=gate[0].rearrange("(q c) -> q c", q=P))
+        load_dy(0)
+        nc.sync.dma_start(offsets[:], offs)
+        load_a(0, 0, 1)
+        load_a(0, 1, 3)
+        load_dy(1)
+        load_a(1, 0, 4)
+        load_dy(2)
+        load_a(2, 0, 4)
+        load_w(0)
+        load_dy(3)
+        load_x(0)
+        load_x(1)
+        load_w(1)
+        load_w(2)
+        load_a(3, 0, 4)
+        load_w(3)
+
+        spread_gate()
+        activations(0, (0, 1, 4))
+        for t in range(PACK - 1):
+            gather_dy(t, 0, 2 * C)
+            gather_dy(t, 2 * C, 2 * C)
+        activations(1)
+        activations(2)
+        qw = weights(0)
+        gather_dy(PACK - 1, 0, C)
+        qg = grads(0)
+        gather_dy(PACK - 1, C, C)
+        qw()
+        qg()
+        gather_dy(PACK - 1, 2 * C, 2 * C)
+        cast_x(0)
+        cast_x(1)
+        slope(0, 0)
+        slope(0, 1)
+        grads(1)()
+        gather_x(0)
+        weights(1)()
+        gather_x(1)
+        grads(2)()
+        weights(2)()
+        collect(0, 0)
+        collect(0, 1)
+        slope(1, 0)
+        slope(1, 1)
+        activations(3)
+        qg = grads(3)
+        qw = weights(3)
+        tokens(0)
+        collect(1, 0)
+        collect(1, 1)
+        slope(2, 0)
+        slope(2, 1)
+        qg()
+        qw()
+        tokens(1)
+        tokens(2)
+        tokens(3)
+        back(0)
+        collect(2, 0)
+        collect(2, 1)
+        slope(3, 0)
+        back(1)
+        collect(3, 0)
+        slope(3, 1)
+        back(2)
+        back(3)

@@ -19,7 +19,7 @@ ACT = mybir.ActivationFunctionType
 P = 128
 PACK = 4
 LIST = 16
-G_ON_VECTOR = ()
+G_ON_VECTOR = (0, 3)
 
 
 def tile_moe_mlp_silu_kernel(tc, xT, dyT, a, w2, gate, offs, out):
@@ -37,7 +37,7 @@ def tile_moe_mlp_silu_kernel(tc, xT, dyT, a, w2, gate, offs, out):
             return offsets[:, first // LIST : (first + count) // LIST]
 
         dy = {}
-        gates = held.tile([P, E * C], F32, name="gates")
+        gates = [held.tile([P, 2 * C], F32, name=f"gates{h}") for h in range(2)]
         pre = [held.tile([P, PACK * C], F32, name=f"pre{e}") for e in range(E)]
         g32 = [held.tile([P, PACK, 2 * C], F32, name=f"g32_{h}") for h in range(2)]
         x_pairs = held.tile([P, 2 * T], BF16, name="x_pairs")
@@ -54,15 +54,14 @@ def tile_moe_mlp_silu_kernel(tc, xT, dyT, a, w2, gate, offs, out):
 
         gate_row = held.tile([P, E * C // P], F32, name="gate_row")
 
-        def spread_gate():
-            for r in range(4):
-                spread = psum.tile([P, 4 * P], F32, name="dh" if r < 2 else "acc", bufs=3)
+        def spread_gate(h, copy):
+            for r in range(2):
+                spread = psum.tile([P, 4 * P], F32, name="dh" if h == 0 else "acc", bufs=3)
                 for c in range(4):
-                    column = gate_row[:, 4 * r + c : 4 * r + c + 1].to_broadcast([P, P])
-                    nc.tensor.transpose(spread[:, c * P : (c + 1) * P], column, ident[:])
-                copy = nc.vector.tensor_copy if r % 2 == 0 else nc.scalar.copy
+                    at = 8 * h + 4 * r + c
+                    nc.tensor.transpose(spread[:, c * P : (c + 1) * P], gate_row[:, at : at + 1].to_broadcast([P, P]), ident[:])
                 copy(
-                    out=gates[:].rearrange("p (q r c) -> p r q c", r=4, c=4)[:, r],
+                    out=gates[h][:].rearrange("p (q r c) -> p r q c", r=2, c=4)[:, r],
                     in_=spread[:].rearrange("p (c q) -> p q c", c=4),
                 )
 
@@ -86,15 +85,16 @@ def tile_moe_mlp_silu_kernel(tc, xT, dyT, a, w2, gate, offs, out):
 
         def activations(e, cuts=(0, 4)):
             rest[e] = ring.tile([P, 4 * C], F32, name="rest", bufs=3)
-            for first, last in zip(cuts, cuts[1:]):
-                part = slice(first * C, last * C)
+            parts = [slice(first * C, last * C) for first, last in zip(cuts, cuts[1:])]
+            for part in parts:
                 nc.scalar.activation(rest[e][:, part], pre[e][:, part], ACT.Silu, scale=-1.0)
+            for part in parts:
                 nc.scalar.activation(pre[e][:, part], pre[e][:, part], ACT.Tanh, scale=-0.5)
 
         def gather_dy(t, first, count):
             h, at = divmod(first, 2 * C)
             nc.vector.tensor_tensor(
-                g32[h][:, t, at : at + count], dy[t][:].indirect(slots(first, count)), gates[:, first : first + count], ALU.mult
+                g32[h][:, t, at : at + count], dy[t][:].indirect(slots(first, count)), gates[h][:, at : at + count], ALU.mult
             )
 
         def weave(copy, dst, src):
@@ -215,13 +215,17 @@ def tile_moe_mlp_silu_kernel(tc, xT, dyT, a, w2, gate, offs, out):
                     nc.scalar.activation(part, acc[:], ACT.Copy, scale=0.5)
                 nc.sync.dma_start(out=out[e, cols, :], in_=part)
 
-        nc.sync.dma_start(out=gate_row[:], in_=gate[0].rearrange("(q c) -> q c", q=P))
+        nc.sync.dma_start(
+            out=gate_row[:].rearrange("q (h c) -> q h c", h=2), in_=gate[0].rearrange("(h q c) -> q h c", h=2, q=P)
+        )
         load_dy(0)
         nc.sync.dma_start(offsets[:], offs)
         load_a(0, 0, 1)
-        load_a(0, 1, 3)
+        load_a(0, 1, 1)
+        load_a(0, 2, 2)
         load_dy(1)
-        load_a(1, 0, 4)
+        load_a(1, 0, 2)
+        load_a(1, 2, 2)
         load_dy(2)
         load_a(2, 0, 4)
         load_w(0)
@@ -233,12 +237,13 @@ def tile_moe_mlp_silu_kernel(tc, xT, dyT, a, w2, gate, offs, out):
         load_a(3, 0, 4)
         load_w(3)
 
-        spread_gate()
-        activations(0, (0, 1, 4))
+        spread_gate(0, nc.vector.tensor_copy)
+        spread_gate(1, nc.scalar.copy)
+        activations(0, (0, 1, 2, 4))
         for t in range(PACK - 1):
             gather_dy(t, 0, 2 * C)
             gather_dy(t, 2 * C, 2 * C)
-        activations(1)
+        activations(1, (0, 2, 4))
         activations(2)
         qw = weights(0)
         gather_dy(PACK - 1, 0, C)

@@ -19,7 +19,9 @@ ACT = mybir.ActivationFunctionType
 P = 128
 PACK = 4
 LIST = 16
-G_ON_VECTOR = (0, 3)
+G_ON_VECTOR = (0, 1)
+G_IN_RAW = (1,)
+OUT_ON_VECTOR = ((3, 1),)
 
 
 def tile_moe_mlp_silu_kernel(tc, xT, dyT, a, w2, gate, offs, out):
@@ -38,18 +40,18 @@ def tile_moe_mlp_silu_kernel(tc, xT, dyT, a, w2, gate, offs, out):
 
         dy = {}
         gates = [held.tile([P, 2 * C], F32, name=f"gates{h}") for h in range(2)]
-        pre = [held.tile([P, PACK * C], F32, name=f"pre{e}") for e in range(E)]
+        pre = [held.tile([P, 4 * 2 * C], F32, name=f"pre{h}") for h in range(2)]
+        rest = [held.tile([P, 4 * 2 * C], F32, name=f"rest{h}") for h in range(2)]
         g32 = [held.tile([P, PACK, 2 * C], F32, name=f"g32_{h}") for h in range(2)]
         x_pairs = held.tile([P, 2 * T], BF16, name="x_pairs")
         x_slots = [held.tile([P, 2 * C], U32, name=f"x_slots{h}") for h in range(2)]
         raw = {}
 
         dy_rows = dyT.rearrange("(p t) c -> p t c", t=PACK)
-        a_rows = a.rearrange("(b p) c -> p b c", p=P)
         x_rows = xT.rearrange("(p j) c -> p j c", j=2)
 
         def load_dy(t):
-            dy[t] = ring.tile([P, T], F32, name="raw", bufs=7)
+            dy[t] = ring.tile([P, T], F32, name="raw", bufs=7, align_bytes=64)
             nc.sync.dma_start(out=dy[t][:], in_=dy_rows[:, t, :])
 
         gate_row = held.tile([P, E * C // P], F32, name="gate_row")
@@ -65,31 +67,29 @@ def tile_moe_mlp_silu_kernel(tc, xT, dyT, a, w2, gate, offs, out):
                     in_=spread[:].rearrange("p (c q) -> p q c", c=4),
                 )
 
-        def load_a(e, first, count):
-            nc.sync.dma_start(
-                out=pre[e][:, first * C : (first + count) * C].rearrange("p (b c) -> p b c", b=count),
-                in_=a_rows[:, first : first + count, e * C : (e + 1) * C],
-            )
+        def load_a(h, b):
+            nc.sync.dma_start(out=pre[h][:, b * 2 * C : (b + 1) * 2 * C], in_=a[b * P : (b + 1) * P, h * 2 * C : (h + 1) * 2 * C])
 
         def load_w(e):
-            raw["w", e] = ring.tile([P, PACK * H], F32, name="raw", bufs=7)
+            raw["w", e] = ring.tile([P, PACK * H], F32, name="raw", bufs=7, align_bytes=64)
             nc.sync.dma_start(out=raw["w", e][:], in_=w2[e].rearrange("(p t) i -> p (t i)", t=PACK))
 
         def load_x(h):
-            raw["x", h] = ring.tile([P, T], F32, name="raw", bufs=7)
+            raw["x", h] = ring.tile([P, T], F32, name="raw", bufs=7, align_bytes=64)
             nc.sync.dma_start(
                 out=raw["x", h][:].rearrange("p (j c) -> p j c", j=2), in_=x_rows[:, :, h * T // 2 : (h + 1) * T // 2]
             )
 
-        rest = {}
+        def activations(h, first, count):
+            parts = [slice(b * 2 * C, (b + 1) * 2 * C) for b in range(first, first + count)]
+            for part in parts:
+                nc.scalar.activation(rest[h][:, part], pre[h][:, part], ACT.Silu, scale=-1.0)
+            for part in parts:
+                nc.scalar.activation(pre[h][:, part], pre[h][:, part], ACT.Tanh, scale=-0.5)
 
-        def activations(e, cuts=(0, 4)):
-            rest[e] = ring.tile([P, 4 * C], F32, name="rest", bufs=3)
-            parts = [slice(first * C, last * C) for first, last in zip(cuts, cuts[1:])]
-            for part in parts:
-                nc.scalar.activation(rest[e][:, part], pre[e][:, part], ACT.Silu, scale=-1.0)
-            for part in parts:
-                nc.scalar.activation(pre[e][:, part], pre[e][:, part], ACT.Tanh, scale=-0.5)
+        def of_expert(tiles, e, first, count):
+            rows = tiles[e // 2][:].rearrange("p (b x c) -> p b x c", b=4, x=2)
+            return rows[:, first : first + count, e % 2, :]
 
         def gather_dy(t, first, count):
             h, at = divmod(first, 2 * C)
@@ -118,7 +118,10 @@ def tile_moe_mlp_silu_kernel(tc, xT, dyT, a, w2, gate, offs, out):
             return lambda: wq.update({e: quantise(wb[:], E4M3, "w", 2)})
 
         def grads(e):
-            gb = ring.tile([P, PACK * C], BF16, name="gb", align_bytes=64)
+            if e in G_IN_RAW:
+                gb = raw["w", e - 1][:, : PACK * C // 2].bitcast(BF16)
+            else:
+                gb = ring.tile([P, PACK * C], BF16, name="gb", align_bytes=64)
             h, at = divmod(e * C, 2 * C)
             copy = nc.vector.tensor_copy if e in G_ON_VECTOR else nc.scalar.copy
             weave(copy, gb[:], g32[h][:, :, at : at + C])
@@ -141,8 +144,8 @@ def tile_moe_mlp_silu_kernel(tc, xT, dyT, a, w2, gate, offs, out):
                 nc.tensor.transpose(turned[:, t * P : (t + 1) * P], words[:, at + t : at + C : PACK], ident[:])
             xb = ring.tile([P, PACK * K], BF16, name="xb", align_bytes=64)
             nc.scalar.copy(
-                out=xb[:].rearrange("p (k t) -> p k t", t=PACK),
-                in_=turned[:].bitcast(BF16).rearrange("p (t k) -> p k t", t=PACK),
+                out=xb[:].rearrange("p (w j t) -> p w t j", j=2, t=PACK),
+                in_=turned[:].bitcast(BF16).rearrange("p (t w j) -> p w t j", j=2, t=PACK),
             )
             xq[e] = quantise(xb[:], E4M3, "x", 4)
 
@@ -160,16 +163,19 @@ def tile_moe_mlp_silu_kernel(tc, xT, dyT, a, w2, gate, offs, out):
                 )
                 sums.append(dh)
             for b in range(2):
-                part = slice(b * C, (b + 1) * C)
-                nc.vector.scalar_tensor_tensor(
-                    rest[e][:, 2 * h * C :][:, part], rest[e][:, 2 * h * C :][:, part], 1.0, sums[b][:], ALU.subtract, ALU.mult
-                )
+                part = of_expert(rest, e, 2 * h + b, 1)[:, 0, :]
+                nc.vector.scalar_tensor_tensor(part, part, 1.0, sums[b][:], ALU.subtract, ALU.mult)
             words = da[:].bitcast(F32)
             turned_da[e, h] = []
             for blocks in [(0,), (1,)] if (e, h) == (E - 1, 1) else [(0, 1)]:
                 part = slice(blocks[0] * C, (blocks[-1] + 1) * C)
                 nc.vector.scalar_tensor_tensor(
-                    da[:, part], pre[e][:, 2 * h * C :][:, part], 1.0, rest[e][:, 2 * h * C :][:, part], ALU.subtract, ALU.mult
+                    da[:, part].rearrange("p (b c) -> p b c", c=C),
+                    of_expert(pre, e, 2 * h + blocks[0], len(blocks)),
+                    1.0,
+                    of_expert(rest, e, 2 * h + blocks[0], len(blocks)),
+                    ALU.subtract,
+                    ALU.mult,
                 )
                 turned = psum.tile([P, 2 * len(blocks) * P], F32, name="da_turned")
                 for b in blocks:
@@ -200,7 +206,7 @@ def tile_moe_mlp_silu_kernel(tc, xT, dyT, a, w2, gate, offs, out):
                     scales=scales[:, cols],
                     in_=da_t[e][:, cols.start * PACK : cols.stop * PACK],
                 )
-            result = ring.tile([P, K // P * H], F32, name="raw", bufs=7)
+            result = ring.tile([P, K // P * H], F32, name="raw", bufs=7, align_bytes=64)
             for kb in range(K // P):
                 cols = slice(kb * P, (kb + 1) * P)
                 part = result[:, kb * H : (kb + 1) * H]
@@ -209,7 +215,7 @@ def tile_moe_mlp_silu_kernel(tc, xT, dyT, a, w2, gate, offs, out):
                     out=acc[:], lhsT=xq[e][0][:, cols].bitcast(E4M3), lhsT_scale=xq[e][1][:, cols],
                     rhs=codes[:].bitcast(E5M2), rhs_scale=scales[:], start=True, stop=True,
                 )
-                if e == E - 1 and kb == 1:
+                if (e, kb) in OUT_ON_VECTOR:
                     nc.vector.tensor_scalar_mul(part, acc[:], 0.5)
                 else:
                     nc.scalar.activation(part, acc[:], ACT.Copy, scale=0.5)
@@ -220,70 +226,73 @@ def tile_moe_mlp_silu_kernel(tc, xT, dyT, a, w2, gate, offs, out):
         )
         load_dy(0)
         nc.sync.dma_start(offsets[:], offs)
-        load_a(0, 0, 1)
-        load_a(0, 1, 1)
-        load_a(0, 2, 2)
+        load_a(0, 0)
+        load_a(0, 1)
         load_dy(1)
-        load_a(1, 0, 2)
-        load_a(1, 2, 2)
+        load_a(0, 2)
+        load_a(0, 3)
         load_dy(2)
-        load_a(2, 0, 4)
-        load_w(0)
+        load_a(1, 0)
+        load_a(1, 1)
         load_dy(3)
+        load_w(0)
+        load_w(1)
         load_x(0)
         load_x(1)
-        load_w(1)
         load_w(2)
-        load_a(3, 0, 4)
+        load_a(1, 2)
+        load_a(1, 3)
         load_w(3)
 
         spread_gate(0, nc.vector.tensor_copy)
         spread_gate(1, nc.scalar.copy)
-        activations(0, (0, 1, 2, 4))
-        for t in range(PACK - 1):
-            gather_dy(t, 0, 2 * C)
-            gather_dy(t, 2 * C, 2 * C)
-        activations(1, (0, 2, 4))
-        activations(2)
+        activations(0, 0, 2)
+        gather_dy(0, 0, 2 * C)
+        gather_dy(0, 2 * C, 2 * C)
+        gather_dy(1, 0, 2 * C)
+        gather_dy(1, 2 * C, 2 * C)
+        gather_dy(2, 0, 2 * C)
+        gather_dy(2, 2 * C, 2 * C)
+        activations(0, 2, 2)
+        activations(1, 0, 2)
         qw = weights(0)
-        gather_dy(PACK - 1, 0, C)
+        gather_dy(3, 0, C)
         qg = grads(0)
-        gather_dy(PACK - 1, C, C)
-        qw()
         qg()
-        gather_dy(PACK - 1, 2 * C, 2 * C)
-        cast_x(0)
-        cast_x(1)
+        gather_dy(3, C, C)
+        qw()
+        gather_dy(3, 2 * C, 2 * C)
+        grads(1)()
+        weights(1)()
         slope(0, 0)
         slope(0, 1)
-        grads(1)()
-        gather_x(0)
-        weights(1)()
-        gather_x(1)
+        cast_x(0)
+        cast_x(1)
         grads(2)()
         weights(2)()
+        activations(1, 2, 2)
+        qg = grads(3)
         collect(0, 0)
         collect(0, 1)
         slope(1, 0)
         slope(1, 1)
-        activations(3)
-        qg = grads(3)
-        qw = weights(3)
+        gather_x(0)
+        gather_x(1)
         tokens(0)
+        tokens(1)
+        qg()
+        weights(3)()
         collect(1, 0)
         collect(1, 1)
         slope(2, 0)
         slope(2, 1)
-        qg()
-        qw()
-        tokens(1)
         tokens(2)
         tokens(3)
         back(0)
         collect(2, 0)
         collect(2, 1)
-        slope(3, 0)
         back(1)
+        slope(3, 0)
         collect(3, 0)
         slope(3, 1)
         back(2)

@@ -5,6 +5,7 @@ from concourse.masks import make_identity
 
 K, T, E, C, H, N = 256, 2048, 4, 512, 512, 512
 FLOPS = 2 * E * C * H * (N + K)
+BYTES = 4 * (K * T + N * T + H * E * C + E * N * H + E * C + E * K * H) + 2 * 128 * (E * C // 16)
 
 F32 = mybir.dt.float32
 BF16 = mybir.dt.bfloat16
@@ -18,10 +19,16 @@ ACT = mybir.ActivationFunctionType
 
 P = 128
 PACK = 4
-LIST = 16
-G_ON_VECTOR = (0, 1)
-G_IN_RAW = (1,)
-OUT_ON_VECTOR = ((3, 1),)
+PER_COLUMN = 16
+PAIR = 2 * C
+BLOCKS = H // P
+LINE = 4
+LAST = E - 1
+
+BIG_BUFS = 7
+DH_BANKS = 3
+SHARED_BANKS = 3
+GATHER_GROUPS = ((0, 1), (1, 1), (2, 2))
 
 
 def tile_moe_mlp_silu_kernel(tc, xT, dyT, a, w2, gate, offs, out):
@@ -31,210 +38,231 @@ def tile_moe_mlp_silu_kernel(tc, xT, dyT, a, w2, gate, offs, out):
         ring = ctx.enter_context(tc.tile_pool(name="ring", bufs=2))
         psum = ctx.enter_context(tc.psum_pool(name="psum", bufs=2))
 
-        offsets = held.tile([P, E * C // LIST], U16, name="offsets")
+        offsets = held.tile([P, E * C // PER_COLUMN], U16, name="offsets")
         ident = held.tile([P, P], F32, name="ident")
         make_identity(nc, ident[:])
 
         def slots(first, count):
-            return offsets[:, first // LIST : (first + count) // LIST]
+            return offsets[:, first // PER_COLUMN : (first + count) // PER_COLUMN]
 
-        dy = {}
-        gates = [held.tile([P, 2 * C], F32, name=f"gates{h}") for h in range(2)]
-        pre = [held.tile([P, 4 * 2 * C], F32, name=f"pre{h}") for h in range(2)]
-        rest = [held.tile([P, 4 * 2 * C], F32, name=f"rest{h}") for h in range(2)]
-        g32 = [held.tile([P, PACK, 2 * C], F32, name=f"g32_{h}") for h in range(2)]
-        x_pairs = held.tile([P, 2 * T], BF16, name="x_pairs")
-        x_slots = [held.tile([P, 2 * C], U32, name=f"x_slots{h}") for h in range(2)]
-        raw = {}
+        def big_tile():
+            return ring.tile([P, T], F32, name="big", bufs=BIG_BUFS, align_bytes=64)
 
-        dy_rows = dyT.rearrange("(p t) c -> p t c", t=PACK)
-        x_rows = xT.rearrange("(p j) c -> p j c", j=2)
+        def dh_bank():
+            return psum.tile([P, C], F32, name="dh", bufs=DH_BANKS)
+
+        def shared_bank():
+            return psum.tile([P, C], F32, name="shared", bufs=SHARED_BANKS)
+
+        gates = [held.tile([P, PAIR], F32, name=f"gates{pair}") for pair in range(2)]
+        tanh_a = [held.tile([P, BLOCKS * PAIR], F32, name=f"tanh_a{pair}") for pair in range(2)]
+        silu_a = [held.tile([P, BLOCKS * PAIR], F32, name=f"silu_a{pair}") for pair in range(2)]
+        g32 = [
+            held.tile([P, PACK * C * count], F32, name=f"g32_{first}", align_bytes=64) for first, count in GATHER_GROUPS
+        ]
+        x_words = held.tile([P, 2 * T], BF16, name="x_words")
+        x_slots = [held.tile([P, PAIR], U32, name=f"x_slots{pair}") for pair in range(2)]
+        gate_row = held.tile([P, E * C // P], F32, name="gate_row")
+        dy, w32, x32 = {}, {}, {}
+
 
         def load_dy(t):
-            dy[t] = ring.tile([P, T], F32, name="raw", bufs=7, align_bytes=64)
-            nc.sync.dma_start(out=dy[t][:], in_=dy_rows[:, t, :])
+            dy[t] = big_tile()
+            nc.sync.dma_start(out=dy[t][:], in_=dyT.rearrange("(p t) c -> p t c", t=PACK)[:, t, :])
 
-        gate_row = held.tile([P, E * C // P], F32, name="gate_row")
-
-        def spread_gate(h, copy):
-            for r in range(2):
-                spread = psum.tile([P, 4 * P], F32, name="dh" if h == 0 else "acc", bufs=3)
-                for c in range(4):
-                    at = 8 * h + 4 * r + c
-                    nc.tensor.transpose(spread[:, c * P : (c + 1) * P], gate_row[:, at : at + 1].to_broadcast([P, P]), ident[:])
-                copy(
-                    out=gates[h][:].rearrange("p (q r c) -> p r q c", r=2, c=4)[:, r],
-                    in_=spread[:].rearrange("p (c q) -> p q c", c=4),
-                )
-
-        def load_a(h, b):
-            nc.sync.dma_start(out=pre[h][:, b * 2 * C : (b + 1) * 2 * C], in_=a[b * P : (b + 1) * P, h * 2 * C : (h + 1) * 2 * C])
+        def load_a(pair, block):
+            nc.sync.dma_start(
+                out=tanh_a[pair][:, block * PAIR : (block + 1) * PAIR],
+                in_=a[block * P : (block + 1) * P, pair * PAIR : (pair + 1) * PAIR],
+            )
 
         def load_w(e):
-            raw["w", e] = ring.tile([P, PACK * H], F32, name="raw", bufs=7, align_bytes=64)
-            nc.sync.dma_start(out=raw["w", e][:], in_=w2[e].rearrange("(p t) i -> p (t i)", t=PACK))
+            w32[e] = big_tile()
+            nc.sync.dma_start(out=w32[e][:], in_=w2[e].rearrange("(p t) i -> p (t i)", t=PACK))
 
-        def load_x(h):
-            raw["x", h] = ring.tile([P, T], F32, name="raw", bufs=7, align_bytes=64)
+        def load_x(part):
+            x32[part] = big_tile()
+            tokens = slice(part * T // 2, (part + 1) * T // 2)
             nc.sync.dma_start(
-                out=raw["x", h][:].rearrange("p (j c) -> p j c", j=2), in_=x_rows[:, :, h * T // 2 : (h + 1) * T // 2]
+                out=x32[part][:].rearrange("p (j c) -> p j c", j=2),
+                in_=xT.rearrange("(p j) c -> p j c", j=2)[:, :, tokens],
             )
 
-        def activations(h, first, count):
-            parts = [slice(b * 2 * C, (b + 1) * 2 * C) for b in range(first, first + count)]
+
+        def spread_gate(pair, bank, copy):
+            for r in range(2):
+                spread = bank()
+                for c in range(LINE):
+                    at = 2 * LINE * pair + LINE * r + c
+                    column = gate_row[:, at : at + 1].to_broadcast([P, P])
+                    nc.tensor.transpose(spread[:, c * P : (c + 1) * P], column, ident[:])
+                copy(
+                    out=gates[pair][:].rearrange("p (q r c) -> p r q c", r=2, c=LINE)[:, r],
+                    in_=spread[:].rearrange("p (c q) -> p q c", c=LINE),
+                )
+
+        def activations(pair, half):
+            parts = [slice(block * PAIR, (block + 1) * PAIR) for block in (2 * half, 2 * half + 1)]
             for part in parts:
-                nc.scalar.activation(rest[h][:, part], pre[h][:, part], ACT.Silu, scale=-1.0)
+                nc.scalar.activation(silu_a[pair][:, part], tanh_a[pair][:, part], ACT.Silu, scale=-1.0)
             for part in parts:
-                nc.scalar.activation(pre[h][:, part], pre[h][:, part], ACT.Tanh, scale=-0.5)
+                nc.scalar.activation(tanh_a[pair][:, part], tanh_a[pair][:, part], ACT.Tanh, scale=-0.5)
 
-        def of_expert(tiles, e, first, count):
-            rows = tiles[e // 2][:].rearrange("p (b x c) -> p b x c", b=4, x=2)
-            return rows[:, first : first + count, e % 2, :]
+        def gather_dy(t):
+            for group, (first, count) in enumerate(GATHER_GROUPS):
+                pair, at = divmod(first * C, PAIR)
+                width = count * C
+                nc.vector.tensor_tensor(
+                    g32[group][:, t * width : (t + 1) * width],
+                    dy[t][:].indirect(slots(first * C, width)),
+                    gates[pair][:, at : at + width],
+                    ALU.mult,
+                )
 
-        def gather_dy(t, first, count):
-            h, at = divmod(first, 2 * C)
-            nc.vector.tensor_tensor(
-                g32[h][:, t, at : at + count], dy[t][:].indirect(slots(first, count)), gates[h][:, at : at + count], ALU.mult
-            )
-
-        def weave(copy, dst, src):
+        def interleave(copy, dst, src):
             copy(
-                out=dst.rearrange("p (c i t) -> p c t i", i=4, t=PACK),
-                in_=src.rearrange("p t (c i) -> p c t i", i=4),
+                out=dst.rearrange("p (c i t) -> p c t i", i=LINE, t=PACK),
+                in_=src.rearrange("p t (c i) -> p c t i", i=LINE),
             )
 
-        def quantise(src, fmt, tag, bufs):
+        def quantise(src, fmt, tag, bufs=2):
             width = src.shape[1] // PACK
             codes = ring.tile([P, width], U32, name=tag + "_codes", align_bytes=64, bufs=bufs)
             scales = ring.tile([P, width], U8, name=tag + "_scales", align_bytes=64, bufs=bufs)
             nc.vector.quantize_mx(out=codes[:].bitcast(fmt), scales=scales[:], in_=src)
             return codes, scales
 
-        wq, gq, xq, da_t = {}, {}, {}, {}
-
-        def weights(e):
-            wb = ring.tile([P, PACK * H], BF16, name="wb", align_bytes=64)
-            weave(nc.scalar.copy, wb[:], raw["w", e][:].rearrange("p (t i) -> p t i", t=PACK))
-            return lambda: wq.update({e: quantise(wb[:], E4M3, "w", 2)})
-
-        def grads(e):
-            if e in G_IN_RAW:
-                gb = raw["w", e - 1][:, : PACK * C // 2].bitcast(BF16)
-            else:
-                gb = ring.tile([P, PACK * C], BF16, name="gb", align_bytes=64)
-            h, at = divmod(e * C, 2 * C)
-            copy = nc.vector.tensor_copy if e in G_ON_VECTOR else nc.scalar.copy
-            weave(copy, gb[:], g32[h][:, :, at : at + C])
-            return lambda: gq.update({e: quantise(gb[:], E5M2, "g", 2)})
-
-        def cast_x(h):
-            nc.scalar.copy(
-                out=x_pairs[:, h * T : (h + 1) * T].rearrange("p (c i j) -> p c j i", i=4, j=2),
-                in_=raw["x", h][:].rearrange("p (j c i) -> p c j i", i=4, j=2),
+        def multiply(bank, stationary, columns, moving):
+            nc.tensor.matmul_mx(
+                out=bank[:],
+                lhsT=stationary[0][:, columns].bitcast(E4M3),
+                lhsT_scale=stationary[1][:, columns],
+                rhs=moving[0][:].bitcast(E5M2),
+                rhs_scale=moving[1][:],
+                start=True,
+                stop=True,
             )
 
-        def gather_x(h):
-            nc.vector.tensor_copy(x_slots[h][:], x_pairs[:].bitcast(U32).indirect(slots(h * 2 * C, 2 * C)))
+        def first_half(tile):
+            return tile[:, : T // 2].bitcast(BF16)
 
-        def tokens(e):
-            h, at = divmod(e * C, 2 * C)
-            words = x_slots[h][:].bitcast(F32)
-            turned = psum.tile([P, PACK * P], F32, name="acc", bufs=3)
+        def second_half(tile):
+            return tile[:, T // 2 :].bitcast(BF16)
+
+        w16, g16, wq, gq, xq, da_turned, da16 = {}, {}, {}, {}, {}, {}, {}
+
+        def interleave_w(e, home=None):
+            w16[e] = ring.tile([P, PACK * H], BF16, name="w16", align_bytes=64)[:] if home is None else home
+            interleave(nc.scalar.copy, w16[e], w32[e][:].rearrange("p (t i) -> p t i", t=PACK))
+
+        def quantise_w(e):
+            wq[e] = quantise(w16[e], E4M3, "w")
+
+        def interleave_g(e, home, copy):
+            group = min(e, len(GATHER_GROUPS) - 1)
+            at = (e - GATHER_GROUPS[group][0]) * C
+            g16[e] = home
+            interleave(copy, home, g32[group][:].rearrange("p (t c) -> p t c", t=PACK)[:, :, at : at + C])
+
+        def quantise_g(e):
+            gq[e] = quantise(g16[e], E5M2, "g")
+
+        def pair_x(part):
+            nc.scalar.copy(
+                out=x_words[:, part * T : (part + 1) * T].rearrange("p (c i j) -> p c j i", i=LINE, j=2),
+                in_=x32[part][:].rearrange("p (j c i) -> p c j i", i=LINE, j=2),
+            )
+
+        def gather_x(pair):
+            nc.vector.tensor_copy(x_slots[pair][:], x_words[:].bitcast(U32).indirect(slots(pair * PAIR, PAIR)))
+
+        def turn_x(e):
+            pair, at = divmod(e * C, PAIR)
+            words = x_slots[pair][:].bitcast(F32)
+            bank = shared_bank()
             for t in range(PACK):
-                nc.tensor.transpose(turned[:, t * P : (t + 1) * P], words[:, at + t : at + C : PACK], ident[:])
-            xb = ring.tile([P, PACK * K], BF16, name="xb", align_bytes=64)
+                nc.tensor.transpose(bank[:, t * P : (t + 1) * P], words[:, at + t : at + C : PACK], ident[:])
+            x16 = ring.tile([P, PACK * K], BF16, name="x16", align_bytes=64)
             nc.scalar.copy(
-                out=xb[:].rearrange("p (w j t) -> p w t j", j=2, t=PACK),
-                in_=turned[:].bitcast(BF16).rearrange("p (t w j) -> p w t j", j=2, t=PACK),
+                out=x16[:].rearrange("p (w j t) -> p w t j", j=2, t=PACK),
+                in_=bank[:].bitcast(BF16).rearrange("p (t w j) -> p w t j", j=2, t=PACK),
             )
-            xq[e] = quantise(xb[:], E4M3, "x", 4)
+            xq[e] = quantise(x16[:], E4M3, "x", bufs=E)
 
-        turned_da = {}
+        def of_expert(tiles, e, first, count):
+            rows = tiles[e // 2][:].rearrange("p (b x c) -> p b x c", b=BLOCKS, x=2)
+            return rows[:, first : first + count, e % 2, :]
 
-        def slope(e, h):
+        def make_da(e, half):
             da = ring.tile([P, 2 * C], BF16, name="da", bufs=4)
             sums = []
+            for block in (2 * half, 2 * half + 1):
+                sums.append(dh_bank())
+                multiply(sums[-1], wq[e], slice(block * P, (block + 1) * P), gq[e])
             for b in range(2):
-                cols = slice((2 * h + b) * P, (2 * h + b + 1) * P)
-                dh = psum.tile([P, C], F32, name="dh", bufs=3)
-                nc.tensor.matmul_mx(
-                    out=dh[:], lhsT=wq[e][0][:, cols].bitcast(E4M3), lhsT_scale=wq[e][1][:, cols],
-                    rhs=gq[e][0][:].bitcast(E5M2), rhs_scale=gq[e][1][:], start=True, stop=True,
-                )
-                sums.append(dh)
-            for b in range(2):
-                part = of_expert(rest, e, 2 * h + b, 1)[:, 0, :]
+                part = of_expert(silu_a, e, 2 * half + b, 1)[:, 0, :]
                 nc.vector.scalar_tensor_tensor(part, part, 1.0, sums[b][:], ALU.subtract, ALU.mult)
             words = da[:].bitcast(F32)
-            turned_da[e, h] = []
-            for blocks in [(0,), (1,)] if (e, h) == (E - 1, 1) else [(0, 1)]:
-                part = slice(blocks[0] * C, (blocks[-1] + 1) * C)
+            is_last = (e, half) == (LAST, 1)
+            for first, count in ((0, 1), (1, 1)) if is_last else ((0, 2),):
                 nc.vector.scalar_tensor_tensor(
-                    da[:, part].rearrange("p (b c) -> p b c", c=C),
-                    of_expert(pre, e, 2 * h + blocks[0], len(blocks)),
+                    da[:, first * C : (first + count) * C].rearrange("p (b c) -> p b c", c=C),
+                    of_expert(tanh_a, e, 2 * half + first, count),
                     1.0,
-                    of_expert(rest, e, 2 * h + blocks[0], len(blocks)),
+                    of_expert(silu_a, e, 2 * half + first, count),
                     ALU.subtract,
                     ALU.mult,
                 )
-                turned = psum.tile([P, 2 * len(blocks) * P], F32, name="da_turned")
-                for b in blocks:
+                bank = psum.tile([P, 2 * count * P], F32, name="da_turned")
+                for b in range(count):
                     for u in range(2):
-                        q = 2 * (b - blocks[0]) + u
+                        start = (first + b) * C // 2
                         nc.tensor.transpose(
-                            turned[:, q * P : (q + 1) * P], words[:, b * C // 2 + u : (b + 1) * C // 2 : 2], ident[:]
+                            bank[:, (2 * b + u) * P : (2 * b + u + 1) * P], words[:, start + u : start + C // 2 : 2], ident[:]
                         )
-                turned_da[e, h].append((2 * h + blocks[0], len(blocks), turned))
-                if len(blocks) == 1:
-                    collect(e, h)
+                da_turned[e, half] = (bank, 2 * half + first, count)
+                if is_last:
+                    collect_da(e, half)
 
-        def collect(e, h):
-            if h == 0:
-                da_t[e] = ring.tile([P, PACK * H], BF16, name="da_t", align_bytes=64)
-            first, count, turned = turned_da[e, h].pop()
+        def collect_da(e, half):
+            if e not in da16:
+                da16[e] = ring.tile([P, PACK * H], BF16, name="da16", align_bytes=64)[:]
+            bank, block, count = da_turned[e, half]
+            words = da16[e][:, block * PACK * P : (block + count) * PACK * P].bitcast(F32)
             nc.scalar.copy(
-                out=da_t[e][:, first * PACK * P : (first + count) * PACK * P].bitcast(F32).rearrange("p (b i u) -> p b i u", i=P, u=2),
-                in_=turned[:].rearrange("p (b u i) -> p b i u", i=P, u=2),
+                out=words.rearrange("p (b c i u) -> p b c u i", c=P // 2, i=2, u=2),
+                in_=bank[:].rearrange("p (b u c i) -> p b c u i", c=P // 2, i=2, u=2),
             )
 
-        def back(e):
+        def finish(e):
             codes = ring.tile([P, H], U32, name="da_codes", align_bytes=64)
             scales = ring.tile([P, H], U8, name="da_scales", align_bytes=64)
-            for cols in [slice(0, 2 * P), slice(2 * P, 3 * P), slice(3 * P, H)] if e == E - 1 else [slice(0, H)]:
+            cuts = (0, 2 * P, 3 * P, H) if e == LAST else (0, H)
+            for lo, hi in zip(cuts, cuts[1:]):
                 nc.vector.quantize_mx(
-                    out=codes[:, cols].bitcast(E5M2),
-                    scales=scales[:, cols],
-                    in_=da_t[e][:, cols.start * PACK : cols.stop * PACK],
+                    out=codes[:, lo:hi].bitcast(E5M2), scales=scales[:, lo:hi], in_=da16[e][:, lo * PACK : hi * PACK]
                 )
-            result = ring.tile([P, K // P * H], F32, name="raw", bufs=7, align_bytes=64)
+            result = big_tile()
             for kb in range(K // P):
-                cols = slice(kb * P, (kb + 1) * P)
+                rows = slice(kb * P, (kb + 1) * P)
                 part = result[:, kb * H : (kb + 1) * H]
-                acc = psum.tile([P, H], F32, name="dh", bufs=3) if e == E - 1 else psum.tile([P, H], F32, name="acc", bufs=3)
-                nc.tensor.matmul_mx(
-                    out=acc[:], lhsT=xq[e][0][:, cols].bitcast(E4M3), lhsT_scale=xq[e][1][:, cols],
-                    rhs=codes[:].bitcast(E5M2), rhs_scale=scales[:], start=True, stop=True,
-                )
-                if (e, kb) in OUT_ON_VECTOR:
-                    nc.vector.tensor_scalar_mul(part, acc[:], 0.5)
+                bank = dh_bank() if e == LAST else shared_bank()
+                multiply(bank, xq[e], rows, (codes, scales))
+                if (e, kb) == (LAST, 1):
+                    nc.vector.tensor_scalar_mul(part, bank[:], 0.5)
                 else:
-                    nc.scalar.activation(part, acc[:], ACT.Copy, scale=0.5)
-                nc.sync.dma_start(out=out[e, cols, :], in_=part)
+                    nc.scalar.activation(part, bank[:], ACT.Copy, scale=0.5)
+                nc.sync.dma_start(out=out[e, rows, :], in_=part)
 
         nc.sync.dma_start(
             out=gate_row[:].rearrange("q (h c) -> q h c", h=2), in_=gate[0].rearrange("(h q c) -> q h c", h=2, q=P)
         )
         load_dy(0)
         nc.sync.dma_start(offsets[:], offs)
-        load_a(0, 0)
-        load_a(0, 1)
-        load_dy(1)
-        load_a(0, 2)
-        load_a(0, 3)
-        load_dy(2)
-        load_a(1, 0)
-        load_a(1, 1)
-        load_dy(3)
+        for t, (pair, half) in enumerate(((0, 0), (0, 1), (1, 0))):
+            load_a(pair, 2 * half)
+            load_a(pair, 2 * half + 1)
+            load_dy(t + 1)
         load_w(0)
         load_w(1)
         load_x(0)
@@ -244,56 +272,60 @@ def tile_moe_mlp_silu_kernel(tc, xT, dyT, a, w2, gate, offs, out):
         load_a(1, 3)
         load_w(3)
 
-        spread_gate(0, nc.vector.tensor_copy)
-        spread_gate(1, nc.scalar.copy)
-        activations(0, 0, 2)
-        gather_dy(0, 0, 2 * C)
-        gather_dy(0, 2 * C, 2 * C)
-        gather_dy(1, 0, 2 * C)
-        gather_dy(1, 2 * C, 2 * C)
-        gather_dy(2, 0, 2 * C)
-        gather_dy(2, 2 * C, 2 * C)
-        activations(0, 2, 2)
-        activations(1, 0, 2)
-        qw = weights(0)
-        gather_dy(3, 0, C)
-        qg = grads(0)
-        qg()
-        gather_dy(3, C, C)
-        qw()
-        gather_dy(3, 2 * C, 2 * C)
-        grads(1)()
-        weights(1)()
-        slope(0, 0)
-        slope(0, 1)
-        cast_x(0)
-        cast_x(1)
-        grads(2)()
-        weights(2)()
-        activations(1, 2, 2)
-        qg = grads(3)
-        collect(0, 0)
-        collect(0, 1)
-        slope(1, 0)
-        slope(1, 1)
+        spread_gate(0, dh_bank, nc.vector.tensor_copy)
+        spread_gate(1, shared_bank, nc.scalar.copy)
+        activations(0, 0)
+        for t in range(PACK - 1):
+            gather_dy(t)
+        activations(0, 1)
+        activations(1, 0)
+        interleave_w(0)
+        gather_dy(PACK - 1)
+
+        quantise_w(0)
+        interleave_g(0, first_half(w32[0]), nc.scalar.copy)
+        quantise_g(0)
+        interleave_g(1, first_half(w32[0]), nc.vector.tensor_copy)
+        quantise_g(1)
+        interleave_w(1, first_half(g32[0]))
+        quantise_w(1)
+
+        make_da(0, 0)
+        make_da(0, 1)
+        pair_x(0)
+        pair_x(1)
+        interleave_g(2, first_half(x32[1]), nc.scalar.copy)
+        quantise_g(2)
+        interleave_w(2)
+        quantise_w(2)
+        activations(1, 1)
+        interleave_g(3, first_half(w32[2]), nc.scalar.copy)
+        da16[0] = second_half(w32[2])
+        collect_da(0, 0)
+        collect_da(0, 1)
+        make_da(1, 0)
+        make_da(1, 1)
+
         gather_x(0)
         gather_x(1)
-        tokens(0)
-        tokens(1)
-        qg()
-        weights(3)()
-        collect(1, 0)
-        collect(1, 1)
-        slope(2, 0)
-        slope(2, 1)
-        tokens(2)
-        tokens(3)
-        back(0)
-        collect(2, 0)
-        collect(2, 1)
-        back(1)
-        slope(3, 0)
-        collect(3, 0)
-        slope(3, 1)
-        back(2)
-        back(3)
+        turn_x(0)
+        turn_x(1)
+        quantise_g(3)
+        interleave_w(3)
+        quantise_w(3)
+        turn_x(2)
+        turn_x(3)
+
+        collect_da(1, 0)
+        collect_da(1, 1)
+        make_da(2, 0)
+        make_da(2, 1)
+        collect_da(2, 0)
+        collect_da(2, 1)
+        make_da(3, 0)
+        finish(0)
+        finish(1)
+        collect_da(3, 0)
+        make_da(3, 1)
+        finish(2)
+        finish(3)

from contextlib import ExitStack

import concourse.mybir as mybir
from concourse.masks import make_identity

K, T, E, C, H, N = 256, 2048, 4, 512, 512, 512
FLOPS = 2 * E * C * H * (N + K)
BYTES = 4 * (K * T + N * T + H * E * C + E * N * H + E * C + E * K * H) + 2 * 128 * (E * C // 16)

F32 = mybir.dt.float32
BF16 = mybir.dt.bfloat16
U32 = mybir.dt.uint32
U16 = mybir.dt.uint16
U8 = mybir.dt.uint8
E4M3 = mybir.dt.float8_e4m3fn_x4
E5M2 = mybir.dt.float8_e5m2_x4
ALU = mybir.AluOpType
ACT = mybir.ActivationFunctionType

P = 128
PACK = 4
PER_COLUMN = 16
PAIR = 2 * C
BLOCKS = H // P
LINE = 4
LAST = E - 1

BIG_BUFS = 7
DH_BANKS = 3
SHARED_BANKS = 3
GATHER_GROUPS = ((0, 1), (1, 1), (2, 2))


def tile_moe_mlp_silu_kernel(tc, xT, dyT, a, w2, gate, offs, out):
    nc = tc.nc
    with ExitStack() as ctx:
        held = ctx.enter_context(tc.tile_pool(name="held", bufs=1))
        ring = ctx.enter_context(tc.tile_pool(name="ring", bufs=2))
        psum = ctx.enter_context(tc.psum_pool(name="psum", bufs=2))

        offsets = held.tile([P, E * C // PER_COLUMN], U16, name="offsets")
        ident = held.tile([P, P], F32, name="ident")
        make_identity(nc, ident[:])

        def slots(first, count):
            return offsets[:, first // PER_COLUMN : (first + count) // PER_COLUMN]

        def big_tile():
            return ring.tile([P, T], F32, name="big", bufs=BIG_BUFS, align_bytes=64)

        def dh_bank():
            return psum.tile([P, C], F32, name="dh", bufs=DH_BANKS)

        def shared_bank():
            return psum.tile([P, C], F32, name="shared", bufs=SHARED_BANKS)

        gates = [held.tile([P, PAIR], F32, name=f"gates{pair}") for pair in range(2)]
        tanh_a = [held.tile([P, BLOCKS * PAIR], F32, name=f"tanh_a{pair}") for pair in range(2)]
        silu_a = [held.tile([P, BLOCKS * PAIR], F32, name=f"silu_a{pair}") for pair in range(2)]
        g32 = [
            held.tile([P, PACK * C * count], F32, name=f"g32_{first}", align_bytes=64) for first, count in GATHER_GROUPS
        ]
        x_words = held.tile([P, 2 * T], BF16, name="x_words")
        x_slots = [held.tile([P, PAIR], U32, name=f"x_slots{pair}") for pair in range(2)]
        gate_row = held.tile([P, E * C // P], F32, name="gate_row")
        dy, w32, x32 = {}, {}, {}


        def load_dy(t):
            dy[t] = big_tile()
            nc.sync.dma_start(out=dy[t][:], in_=dyT.rearrange("(p t) c -> p t c", t=PACK)[:, t, :])

        def load_a(pair, block):
            nc.sync.dma_start(
                out=tanh_a[pair][:, block * PAIR : (block + 1) * PAIR],
                in_=a[block * P : (block + 1) * P, pair * PAIR : (pair + 1) * PAIR],
            )

        def load_w(e):
            w32[e] = big_tile()
            nc.sync.dma_start(out=w32[e][:], in_=w2[e].rearrange("(p t) i -> p (t i)", t=PACK))

        def load_x(part):
            x32[part] = big_tile()
            tokens = slice(part * T // 2, (part + 1) * T // 2)
            nc.sync.dma_start(
                out=x32[part][:].rearrange("p (j c) -> p j c", j=2),
                in_=xT.rearrange("(p j) c -> p j c", j=2)[:, :, tokens],
            )


        def spread_gate(pair, bank, copy):
            for r in range(2):
                spread = bank()
                for c in range(LINE):
                    at = 2 * LINE * pair + LINE * r + c
                    column = gate_row[:, at : at + 1].to_broadcast([P, P])
                    nc.tensor.transpose(spread[:, c * P : (c + 1) * P], column, ident[:])
                copy(
                    out=gates[pair][:].rearrange("p (q r c) -> p r q c", r=2, c=LINE)[:, r],
                    in_=spread[:].rearrange("p (c q) -> p q c", c=LINE),
                )

        def activations(pair, half):
            parts = [slice(block * PAIR, (block + 1) * PAIR) for block in (2 * half, 2 * half + 1)]
            for part in parts:
                nc.scalar.activation(silu_a[pair][:, part], tanh_a[pair][:, part], ACT.Silu, scale=-1.0)
            for part in parts:
                nc.scalar.activation(tanh_a[pair][:, part], tanh_a[pair][:, part], ACT.Tanh, scale=-0.5)

        def gather_dy(t):
            for group, (first, count) in enumerate(GATHER_GROUPS):
                pair, at = divmod(first * C, PAIR)
                width = count * C
                nc.vector.tensor_tensor(
                    g32[group][:, t * width : (t + 1) * width],
                    dy[t][:].indirect(slots(first * C, width)),
                    gates[pair][:, at : at + width],
                    ALU.mult,
                )

        def interleave(copy, dst, src):
            copy(
                out=dst.rearrange("p (c i t) -> p c t i", i=LINE, t=PACK),
                in_=src.rearrange("p t (c i) -> p c t i", i=LINE),
            )

        def quantise(src, fmt, tag, bufs=2):
            width = src.shape[1] // PACK
            codes = ring.tile([P, width], U32, name=tag + "_codes", align_bytes=64, bufs=bufs)
            scales = ring.tile([P, width], U8, name=tag + "_scales", align_bytes=64, bufs=bufs)
            nc.vector.quantize_mx(out=codes[:].bitcast(fmt), scales=scales[:], in_=src)
            return codes, scales

        def multiply(bank, stationary, columns, moving):
            nc.tensor.matmul_mx(
                out=bank[:],
                lhsT=stationary[0][:, columns].bitcast(E4M3),
                lhsT_scale=stationary[1][:, columns],
                rhs=moving[0][:].bitcast(E5M2),
                rhs_scale=moving[1][:],
                start=True,
                stop=True,
            )

        def first_half(tile):
            return tile[:, : T // 2].bitcast(BF16)

        def second_half(tile):
            return tile[:, T // 2 :].bitcast(BF16)

        w16, g16, wq, gq, xq, da_turned, da16 = {}, {}, {}, {}, {}, {}, {}

        def interleave_w(e, home=None):
            w16[e] = ring.tile([P, PACK * H], BF16, name="w16", align_bytes=64)[:] if home is None else home
            interleave(nc.scalar.copy, w16[e], w32[e][:].rearrange("p (t i) -> p t i", t=PACK))

        def quantise_w(e):
            wq[e] = quantise(w16[e], E4M3, "w")

        def interleave_g(e, home, copy):
            group = min(e, len(GATHER_GROUPS) - 1)
            at = (e - GATHER_GROUPS[group][0]) * C
            g16[e] = home
            interleave(copy, home, g32[group][:].rearrange("p (t c) -> p t c", t=PACK)[:, :, at : at + C])

        def quantise_g(e):
            gq[e] = quantise(g16[e], E5M2, "g")

        def pair_x(part):
            nc.scalar.copy(
                out=x_words[:, part * T : (part + 1) * T].rearrange("p (c i j) -> p c j i", i=LINE, j=2),
                in_=x32[part][:].rearrange("p (j c i) -> p c j i", i=LINE, j=2),
            )

        def gather_x(pair):
            nc.vector.tensor_copy(x_slots[pair][:], x_words[:].bitcast(U32).indirect(slots(pair * PAIR, PAIR)))

        def turn_x(e):
            pair, at = divmod(e * C, PAIR)
            words = x_slots[pair][:].bitcast(F32)
            bank = shared_bank()
            for t in range(PACK):
                nc.tensor.transpose(bank[:, t * P : (t + 1) * P], words[:, at + t : at + C : PACK], ident[:])
            x16 = ring.tile([P, PACK * K], BF16, name="x16", align_bytes=64)
            nc.scalar.copy(
                out=x16[:].rearrange("p (w j t) -> p w t j", j=2, t=PACK),
                in_=bank[:].bitcast(BF16).rearrange("p (t w j) -> p w t j", j=2, t=PACK),
            )
            xq[e] = quantise(x16[:], E4M3, "x", bufs=E)

        def of_expert(tiles, e, first, count):
            rows = tiles[e // 2][:].rearrange("p (b x c) -> p b x c", b=BLOCKS, x=2)
            return rows[:, first : first + count, e % 2, :]

        def make_da(e, half):
            da = ring.tile([P, 2 * C], BF16, name="da", bufs=4)
            sums = []
            for block in (2 * half, 2 * half + 1):
                sums.append(dh_bank())
                multiply(sums[-1], wq[e], slice(block * P, (block + 1) * P), gq[e])
            for b in range(2):
                part = of_expert(silu_a, e, 2 * half + b, 1)[:, 0, :]
                nc.vector.scalar_tensor_tensor(part, part, 1.0, sums[b][:], ALU.subtract, ALU.mult)
            words = da[:].bitcast(F32)
            is_last = (e, half) == (LAST, 1)
            for first, count in ((0, 1), (1, 1)) if is_last else ((0, 2),):
                nc.vector.scalar_tensor_tensor(
                    da[:, first * C : (first + count) * C].rearrange("p (b c) -> p b c", c=C),
                    of_expert(tanh_a, e, 2 * half + first, count),
                    1.0,
                    of_expert(silu_a, e, 2 * half + first, count),
                    ALU.subtract,
                    ALU.mult,
                )
                bank = psum.tile([P, 2 * count * P], F32, name="da_turned")
                for b in range(count):
                    for u in range(2):
                        start = (first + b) * C // 2
                        nc.tensor.transpose(
                            bank[:, (2 * b + u) * P : (2 * b + u + 1) * P], words[:, start + u : start + C // 2 : 2], ident[:]
                        )
                da_turned[e, half] = (bank, 2 * half + first, count)
                if is_last:
                    collect_da(e, half)

        def collect_da(e, half):
            if e not in da16:
                da16[e] = ring.tile([P, PACK * H], BF16, name="da16", align_bytes=64)[:]
            bank, block, count = da_turned[e, half]
            words = da16[e][:, block * PACK * P : (block + count) * PACK * P].bitcast(F32)
            nc.scalar.copy(
                out=words.rearrange("p (b c i u) -> p b c u i", c=P // 2, i=2, u=2),
                in_=bank[:].rearrange("p (b u c i) -> p b c u i", c=P // 2, i=2, u=2),
            )

        def finish(e):
            codes = ring.tile([P, H], U32, name="da_codes", align_bytes=64)
            scales = ring.tile([P, H], U8, name="da_scales", align_bytes=64)
            cuts = (0, 2 * P, 3 * P, H) if e == LAST else (0, H)
            for lo, hi in zip(cuts, cuts[1:]):
                nc.vector.quantize_mx(
                    out=codes[:, lo:hi].bitcast(E5M2), scales=scales[:, lo:hi], in_=da16[e][:, lo * PACK : hi * PACK]
                )
            result = big_tile()
            for kb in range(K // P):
                rows = slice(kb * P, (kb + 1) * P)
                part = result[:, kb * H : (kb + 1) * H]
                bank = dh_bank() if e == LAST else shared_bank()
                multiply(bank, xq[e], rows, (codes, scales))
                if (e, kb) == (LAST, 1):
                    nc.vector.tensor_scalar_mul(part, bank[:], 0.5)
                else:
                    nc.scalar.activation(part, bank[:], ACT.Copy, scale=0.5)
                nc.sync.dma_start(out=out[e, rows, :], in_=part)

        nc.sync.dma_start(
            out=gate_row[:].rearrange("q (h c) -> q h c", h=2), in_=gate[0].rearrange("(h q c) -> q h c", h=2, q=P)
        )
        load_dy(0)
        nc.sync.dma_start(offsets[:], offs)
        for t, (pair, half) in enumerate(((0, 0), (0, 1), (1, 0))):
            load_a(pair, 2 * half)
            load_a(pair, 2 * half + 1)
            load_dy(t + 1)
        load_w(0)
        load_w(1)
        load_x(0)
        load_x(1)
        load_w(2)
        load_a(1, 2)
        load_a(1, 3)
        load_w(3)

        spread_gate(0, dh_bank, nc.vector.tensor_copy)
        spread_gate(1, shared_bank, nc.scalar.copy)
        activations(0, 0)
        for t in range(PACK - 1):
            gather_dy(t)
        activations(0, 1)
        activations(1, 0)
        interleave_w(0)
        gather_dy(PACK - 1)

        quantise_w(0)
        interleave_g(0, first_half(w32[0]), nc.scalar.copy)
        quantise_g(0)
        interleave_g(1, first_half(w32[0]), nc.vector.tensor_copy)
        quantise_g(1)
        interleave_w(1, first_half(g32[0]))
        quantise_w(1)

        make_da(0, 0)
        make_da(0, 1)
        pair_x(0)
        pair_x(1)
        interleave_g(2, first_half(x32[1]), nc.scalar.copy)
        quantise_g(2)
        interleave_w(2)
        quantise_w(2)
        activations(1, 1)
        interleave_g(3, first_half(w32[2]), nc.scalar.copy)
        da16[0] = second_half(w32[2])
        collect_da(0, 0)
        collect_da(0, 1)
        make_da(1, 0)
        make_da(1, 1)

        gather_x(0)
        gather_x(1)
        turn_x(0)
        turn_x(1)
        quantise_g(3)
        interleave_w(3)
        quantise_w(3)
        turn_x(2)
        turn_x(3)

        collect_da(1, 0)
        collect_da(1, 1)
        make_da(2, 0)
        make_da(2, 1)
        collect_da(2, 0)
        collect_da(2, 1)
        make_da(3, 0)
        finish(0)
        finish(1)
        collect_da(3, 0)
        make_da(3, 1)
        finish(2)
        finish(3)
